import numpy as np
import ml_dtypes


def mxq(x, axis, fmt="e4m3"):
    dtype, down = {"e4m3": (ml_dtypes.float8_e4m3fn, 7), "e5m2": (ml_dtypes.float8_e5m2, 14)}[fmt]
    v = np.moveaxis(np.asarray(x, np.float32).astype(ml_dtypes.bfloat16).astype(np.float64), axis, -1)
    blocks = v.reshape(v.shape[:-1] + (-1, 32))
    amax = np.abs(blocks).max(-1, keepdims=True)
    byte = np.maximum(np.where(amax > 0, np.frexp(amax)[1] - 1 + 127, 0) - down, 1)
    scale = np.exp2(byte - 127.0)
    codes = (blocks / scale).astype(np.float32).astype(dtype).astype(np.float64)
    return np.moveaxis((codes * scale).reshape(v.shape), -1, axis)


WIDE = False


def mx_kscale(k):
    if not WIDE:
        return np.ones(k)
    levels = np.array([10, -10, 5, -5, 0])
    if k % 512:
        return np.exp2(np.random.permutation(np.resize(levels, k // 32))).repeat(32)
    a = np.empty((k // 512, 16))
    for p in range(k // 512):
        a[p, :8] = np.random.permutation(np.resize(levels, 8))
        for g in range(8):
            far = levels[np.abs(levels - a[p, g]) >= 10]
            a[p, g + 8] = far[np.random.randint(len(far))]
    return np.exp2(a.ravel()).repeat(32)


def f64(x):
    return np.asarray(x).astype(np.float64)


def striped(idx):
    return np.tile(idx.reshape(-1, 16).T, (8, 1)).astype(np.uint16)


def unstriped(offs):
    return offs[:16].T.reshape(-1).astype(np.int64)


def striped8(idx):
    return np.concatenate([x.reshape(-1, 16).T for x in idx]).astype(np.uint16)


def runs(offs, k):
    lists = np.stack([offs[16 * r : 16 * r + 16].T.reshape(-1) for r in range(8)]).astype(np.int64)
    return lists[np.arange(k) % 512 // 64]


def pack_weight(w):
    k, n = w.shape
    w = f64(np.asarray(w, np.float32).astype(ml_dtypes.bfloat16)).reshape(k // 32, 32, n)
    amax = np.abs(w).max(1)
    byte = np.clip(np.where(amax > 0, np.frexp(amax)[1] - 1 + 127 - 7, 1), 1, 254)
    scaled = (w * np.exp2(127.0 - byte)[:, None, :]).reshape(k, n).astype(np.float32)
    words = np.ascontiguousarray(scaled.reshape(k // 512, 128, 4, n).transpose(0, 1, 3, 2)).astype(ml_dtypes.float8_e4m3fn).view(np.uint8)
    return words, np.ascontiguousarray(byte.astype(np.uint8).reshape(k // 512, 16, n))


def unpack_weight(words, scales):
    g, p, n, _ = words.shape
    vals = np.ascontiguousarray(words).view(ml_dtypes.float8_e4m3fn).astype(np.float64) * np.repeat(np.exp2(scales.astype(np.float64) - 127.0), 8, axis=1)[..., None]
    return vals.transpose(0, 1, 3, 2).reshape(g * 512, n)


def sigmoid(v):
    return 1.0 / (1.0 + np.exp(-np.maximum(v, -700.0)))


K, T, S, N, H, J = 512, 2048, 512, 512, 512, 512


def setup_inputs():
    n = np.random.standard_normal
    s = mx_kscale(K)[:, None]
    u = mx_kscale(H)
    packed_xT = pack_weight(n((K, T)) * s)
    return {
        "x_words": packed_xT[0],
        "x_scales": packed_xT[1],
        "w1": (n((K, H)) / np.sqrt(K) / s).astype(np.float32),
        "tab": n((H, J)).astype(np.float32),
        "gn": (np.random.uniform(0.5, 1.5, (H, 1)) * u[:, None]).astype(np.float32),
        "w2": (n((H, N)) / np.sqrt(H) / u[:, None]).astype(np.float32),
        "gm": (np.random.uniform(0.5, 1.5, (H, 1)) * u[:, None]).astype(np.float32),
        "w3": (n((H, N)) / np.sqrt(H) / u[:, None]).astype(np.float32),
        "offs": striped(np.random.permutation(T)[:S]),
        "n1": striped8(np.random.randint(0, J, (8, S))),
        "n2": striped8(np.stack([np.random.permutation(S) for _ in range(8)])),
        "n3": striped8(np.stack([np.random.permutation(S) for _ in range(8)])),
        "n4": striped8(np.stack([np.random.permutation(S) for _ in range(8)])),
        "n5": striped8(np.stack([np.random.permutation(S) for _ in range(8)])),
        "n6": striped8(np.stack([np.random.permutation(S) for _ in range(8)])),
    }


def reference(x_words, x_scales, w1, tab, gn, w2, gm, w3, offs, n1, n2, n3, n4, n5, n6):
    xq = unpack_weight(x_words, x_scales)[:, unstriped(offs)]
    y = mxq(f64(w1), 0, "e4m3").T @ xq
    z = f64(gn) * (np.abs(y - (y[np.arange(H)[:, None], runs(n2, H)]) - (f64(tab)[np.arange(H)[:, None], runs(n1, H)])))
    a = mxq(f64(w2), 0, "e4m3").T @ mxq(z, 0, "e4m3")
    ex = np.exp(y)
    z2 = f64(gm) * (np.log(ex + ex[np.arange(H)[:, None], runs(n3, H)]) - (y[np.arange(H)[:, None], runs(n4, H)]))
    b = mxq(f64(w3), 0, "e4m3").T @ mxq(z2, 0, "e4m3")
    return a + (sigmoid(b[np.arange(N)[:, None], runs(n6, N)] - b)) * (a[np.arange(N)[:, None], runs(n5, N)] - a)

@@ -1,0 +1,183 @@
+from contextlib import ExitStack
+
+import concourse.mybir as mybir
+
+F32 = mybir.dt.float32
+BF16 = mybir.dt.bfloat16
+I32 = mybir.dt.int32
+U32 = mybir.dt.uint32
+U16 = mybir.dt.uint16
+U8 = mybir.dt.uint8
+FP8X4 = mybir.dt.float8_e4m3fn_x4
+ALU = mybir.AluOpType
+ACT = mybir.ActivationFunctionType
+
+P = 128
+PACK = 4
+T = 2048
+S = 512
+W = 512
+FLOPS = 3 * 2 * 512 * 512 * 512
+
+
+def tile_picked_forkpullbkinddlse_none_p_kernel(
+    tc, x_words, x_scales, w1, tab, gn, w2, gm, w3, offs, n1, n2, n3, n4, n5, n6, out
+):
+    nc = tc.nc
+    with ExitStack() as ctx:
+        keep = ctx.enter_context(tc.tile_pool(name="keep", bufs=1))
+        psum = ctx.enter_context(tc.psum_pool(name="psum", bufs=1))
+
+        def load_list(name, src):
+            tile = keep.tile([P, S // 16], U16, name=name)
+            nc.sync.dma_start(tile[:], src)
+            return tile
+
+        def planes(name, width):
+            return [keep.tile([P, width], F32, name=f"{name}{t}") for t in range(PACK)]
+
+        def load_weight(name, w):
+            tile = keep.tile([P, PACK, w.shape[1]], F32, name=f"{name}_raw")
+            nc.sync.dma_start(tile[:], w.rearrange("(p j) n -> p j n", j=PACK))
+            return tile
+
+        def round_weight(name, raw, copy):
+            dealt = keep.tile([P, PACK * W], BF16, name=f"{name}_bf", align_bytes=64)
+            view = dealt[:].rearrange("p (t m j) -> p m j t", t=PACK, j=PACK)
+            span = P // len(raw)
+            for h, tile in enumerate(raw):
+                copy(view[:, h * span : (h + 1) * span], tile[:].rearrange("p j (m t) -> p m j t", t=PACK))
+            return dealt
+
+        def mx_tiles(name):
+            codes = keep.tile([P, W], U32, name=f"{name}_codes", align_bytes=64)
+            scales = keep.tile([P, W], U8, name=f"{name}_scales", align_bytes=64)
+            return codes, scales
+
+        def quantize(mx, values, lo=0, hi=W):
+            nc.vector.quantize_mx(mx[0][:, lo:hi].bitcast(FP8X4), mx[1][:, lo:hi], values[:, PACK * lo : PACK * hi])
+
+        def product(name, tag, weight, moving):
+            banks = []
+            for t in range(PACK):
+                bank = psum.tile([P, S], F32, name=f"{name}{t}", tag=f"{tag}{t}")
+                cols = slice(t * P, (t + 1) * P)
+                nc.tensor.matmul_mx(
+                    bank[:], weight[0][:, cols].bitcast(FP8X4), weight[1][:, cols],
+                    moving[0][:].bitcast(FP8X4), moving[1][:], start=True, stop=True,
+                )
+                banks.append(bank)
+            return banks
+
+        def scale_round_quantize(name, values, gain):
+            rounded = keep.tile([P, PACK * S], BF16, name=f"{name}_bf", align_bytes=64)
+            mx = mx_tiles(name)
+            src = values[:].rearrange("p t (c i) -> p c t i", i=4)
+            dst = rounded[:].rearrange("p (c i t) -> p c t i", i=4, t=PACK)
+            half = S // 8
+            spread = gain[:].unsqueeze(1).unsqueeze(3).broadcast_to([P, half, PACK, 4])
+            for h in range(2):
+                c = slice(h * half, (h + 1) * half)
+                nc.vector.tensor_tensor(dst[:, c], src[:, c], spread, ALU.mult)
+            for h in range(2):
+                quantize(mx, rounded, h * S // 2, (h + 1) * S // 2)
+            return mx
+
+        xs_win = keep.tile([P, T], U8, name="xs_win")
+        nc.vector.memset(xs_win[:].bitcast(I32), 0)
+        gn_sb = keep.tile([P, PACK], F32, name="gn_sb")
+        gm_sb = keep.tile([P, PACK], F32, name="gm_sb")
+        nc.gpsimd.dma_start(gn_sb[:], gn.rearrange("(p t) o -> p (t o)", t=PACK))
+        nc.gpsimd.dma_start(gm_sb[:], gm.rearrange("(p t) o -> p (t o)", t=PACK))
+
+        w1_raw = [load_weight("w1a", w1[:, : W // 2])]
+        for q in range(4):
+            nc.sync.dma_start(xs_win[32 * q : 32 * q + 4, :].bitcast(I32), x_scales[0, 4 * q : 4 * q + 4, :].bitcast(I32))
+        offs_sb = load_list("offs_sb", offs)
+        w1_raw.append(load_weight("w1b", w1[:, W // 2 :]))
+        xw_win = keep.tile([P, T], U32, name="xw_win")
+        nc.sync.dma_start(xw_win[:].bitcast(I32), x_words[0].rearrange("p n t -> p (n t)").bitcast(I32))
+        n1_sb = load_list("n1_sb", n1)
+        n2_sb = load_list("n2_sb", n2)
+        n3_sb = load_list("n3_sb", n3)
+        tab_win = planes("tab_win", 2 * S)
+        tab_rows = tab.rearrange("(p t) n -> p t n", t=PACK)
+        for t in range(PACK):
+            nc.vector.memset(tab_win[t][:, S:], 0.0)
+            nc.sync.dma_start(tab_win[t][:, :S], tab_rows[:, t, :])
+        n4_sb = load_list("n4_sb", n4)
+        w3_raw = [load_weight("w3", w3)]
+        w2_raw = [load_weight("w2", w2)]
+        n6_sb = load_list("n6_sb", n6)
+        n5_sb = load_list("n5_sb", n5)
+
+        neg_gm = keep.tile([P, PACK], F32, name="neg_gm")
+        nc.gpsimd.tensor_scalar(neg_gm[:], gm_sb[:], -1.0, 0.0, ALU.mult, ALU.add)
+
+        w1_mx = mx_tiles("w1")
+        quantize(w1_mx, round_weight("w1", w1_raw, nc.vector.tensor_copy))
+        x_mx = mx_tiles("x")
+        nc.vector.tensor_copy(x_mx[1][:], xs_win[:].indirect(offs_sb[:]))
+        nc.vector.tensor_copy(x_mx[0][:], xw_win[:].indirect(offs_sb[:]))
+        y_ps = product("y_ps", "lo", w1_mx, x_mx)
+
+        y_win = planes("y_win", 2 * S)
+        a_win = planes("a_win", 2 * S)
+        b_win = planes("b_win", 2 * S)
+        lse = planes("lse", S)
+        ex3 = planes("ex3", S)
+        exsum = planes("exsum", S)
+        diff = keep.tile([P, PACK, S], F32, name="diff")
+        size = keep.tile([P, PACK, S], F32, name="size")
+        rest = keep.tile([P, PACK, S], F32, name="rest")
+
+        for pair in ((0, 1), (2, 3)):
+            for t in pair:
+                nc.scalar.copy(y_win[t][:, :S], y_ps[t][:])
+            for t in pair:
+                nc.scalar.activation(y_win[t][:, S:], y_ps[t][:], ACT.Exp)
+            for t in pair:
+                nc.scalar.activation(ex3[t][:], y_win[t][:].indirect(n3_sb[:]), ACT.Exp)
+            for t in pair:
+                nc.vector.tensor_tensor(b_win[t][:, S:], tab_win[t][:].indirect(n1_sb[:]), y_win[t][:, :S], ALU.subtract)
+            for t in pair:
+                nc.vector.tensor_tensor(diff[:, t, :], y_win[t][:].indirect(n2_sb[:]), b_win[t][:, S:], ALU.add)
+            for t in pair:
+                nc.vector.tensor_tensor(exsum[t][:], ex3[t][:], y_win[t][:, S:], ALU.add)
+        for t in range(PACK):
+            nc.scalar.activation(lse[t][:], exsum[t][:], ACT.Ln)
+            nc.vector.tensor_tensor(rest[:, t, :], y_win[t][:].indirect(n4_sb[:]), lse[t][:], ALU.subtract)
+        w3_bf = round_weight("w3", w3_raw, nc.scalar.copy)
+        nc.scalar.activation(size[:], diff[:], ACT.Abs)
+        w2_bf = round_weight("w2", w2_raw, nc.scalar.copy)
+
+        w3_mx = mx_tiles("w3")
+        quantize(w3_mx, w3_bf)
+        z2_mx = scale_round_quantize("z2", rest, neg_gm)
+        b_ps = product("b_ps", "hi", w3_mx, z2_mx)
+        z_mx = scale_round_quantize("z", size, gn_sb)
+        w2_mx = mx_tiles("w2")
+        quantize(w2_mx, w2_bf)
+        a_ps = product("a_ps", "lo", w2_mx, z_mx)
+
+        gap = planes("gap", S)
+        gate = planes("gate", S)
+        far = planes("far", S)
+        near = planes("near", S)
+        res = planes("res", S)
+        out_rows = out.rearrange("(p t) n -> p t n", t=PACK)
+        for t in range(PACK):
+            nc.scalar.copy(b_win[t][:, :S], b_ps[t][:])
+            nc.scalar.copy(a_win[t][:, S:], b_ps[t][:])
+            nc.vector.tensor_tensor(gap[t][:], b_win[t][:].indirect(n6_sb[:]), a_win[t][:, S:], ALU.subtract)
+        for t in range(PACK):
+            nc.scalar.activation(gate[t][:], gap[t][:], ACT.Sigmoid)
+            nc.scalar.copy(a_win[t][:, :S], a_ps[t][:])
+        for t in range(PACK):
+            nc.vector.tensor_tensor(far[t][:], a_win[t][:].indirect(n5_sb[:]), gate[t][:], ALU.mult)
+            nc.vector.scalar_tensor_tensor(near[t][:], gate[t][:], 1.0, a_win[t][:, :S], ALU.subtract, ALU.mult)
+            if t > 0:
+                nc.vector.tensor_tensor(res[t - 1][:], far[t - 1][:], near[t - 1][:], ALU.subtract)
+                nc.sync.dma_start(out_rows[:, t - 1, :], res[t - 1][:])
+        nc.vector.tensor_tensor(res[3][:], far[3][:], near[3][:], ALU.subtract)
+        nc.sync.dma_start(out_rows[:, 3, :], res[3][:])

@@ -84,7 +84,10 @@ def tile_picked_forkpullbkinddlse_none_p_kernel(
             return mx
 
         xs_win = keep.tile([P, T], U8, name="xs_win")
-        nc.vector.memset(xs_win[:].bitcast(I32), 0)
+        nc.gpsimd.memset(xs_win[:].bitcast(I32), 0)
+        tab_win = planes("tab_win", 2 * S)
+        for t in range(PACK):
+            nc.gpsimd.memset(tab_win[t][:, S:], 0.0)
         gn_sb = keep.tile([P, PACK], F32, name="gn_sb")
         gm_sb = keep.tile([P, PACK], F32, name="gm_sb")
         nc.gpsimd.dma_start(gn_sb[:], gn.rearrange("(p t) o -> p (t o)", t=PACK))
@@ -100,19 +103,15 @@ def tile_picked_forkpullbkinddlse_none_p_kernel(
         n1_sb = load_list("n1_sb", n1)
         n2_sb = load_list("n2_sb", n2)
         n3_sb = load_list("n3_sb", n3)
-        tab_win = planes("tab_win", 2 * S)
         tab_rows = tab.rearrange("(p t) n -> p t n", t=PACK)
-        for t in range(PACK):
-            nc.vector.memset(tab_win[t][:, S:], 0.0)
+        for t in (1, 0, 2, 3):
             nc.sync.dma_start(tab_win[t][:, :S], tab_rows[:, t, :])
         n4_sb = load_list("n4_sb", n4)
-        w3_raw = [load_weight("w3", w3)]
-        w2_raw = [load_weight("w2", w2)]
+        w3_raw = load_weight("w3", w3)
+        w2_raw = load_weight("w2", w2)
         n6_sb = load_list("n6_sb", n6)
         n5_sb = load_list("n5_sb", n5)
 
-        neg_gm = keep.tile([P, PACK], F32, name="neg_gm")
-        nc.gpsimd.tensor_scalar(neg_gm[:], gm_sb[:], -1.0, 0.0, ALU.mult, ALU.add)
 
         w1_mx = mx_tiles("w1")
         quantize(w1_mx, round_weight("w1", w1_raw, nc.vector.tensor_copy))
@@ -131,6 +130,8 @@ def tile_picked_forkpullbkinddlse_none_p_kernel(
         size = keep.tile([P, PACK, S], F32, name="size")
         rest = keep.tile([P, PACK, S], F32, name="rest")
 
+        nc.vector.tensor_copy(b_win[1][:, S:], tab_win[1][:].indirect(n1_sb[:]))
+        both = keep.tile([P, S], F32, name="both")
         for pair in ((0, 1), (2, 3)):
             for t in pair:
                 nc.scalar.copy(y_win[t][:, :S], y_ps[t][:])
@@ -139,21 +140,25 @@ def tile_picked_forkpullbkinddlse_none_p_kernel(
             for t in pair:
                 nc.scalar.activation(ex3[t][:], y_win[t][:].indirect(n3_sb[:]), ACT.Exp)
             for t in pair:
-                nc.vector.tensor_tensor(b_win[t][:, S:], tab_win[t][:].indirect(n1_sb[:]), y_win[t][:, :S], ALU.subtract)
+                if t != 1:
+                    nc.vector.tensor_tensor(b_win[t][:, S:], tab_win[t][:].indirect(n1_sb[:]), y_win[t][:, :S], ALU.subtract)
             for t in pair:
-                nc.vector.tensor_tensor(diff[:, t, :], y_win[t][:].indirect(n2_sb[:]), b_win[t][:, S:], ALU.add)
+                dst = both[:] if t == 1 else diff[:, t, :]
+                nc.vector.tensor_tensor(dst, y_win[t][:].indirect(n2_sb[:]), b_win[t][:, S:], ALU.add)
+            if pair[0] == 0:
+                nc.vector.tensor_tensor(diff[:, 1, :], both[:], y_win[1][:, :S], ALU.subtract)
             for t in pair:
                 nc.vector.tensor_tensor(exsum[t][:], ex3[t][:], y_win[t][:, S:], ALU.add)
         for t in range(PACK):
             nc.scalar.activation(lse[t][:], exsum[t][:], ACT.Ln)
             nc.vector.tensor_tensor(rest[:, t, :], y_win[t][:].indirect(n4_sb[:]), lse[t][:], ALU.subtract)
-        w3_bf = round_weight("w3", w3_raw, nc.scalar.copy)
+        w3_bf = round_weight("w3", [w3_raw], nc.scalar.copy)
         nc.scalar.activation(size[:], diff[:], ACT.Abs)
-        w2_bf = round_weight("w2", w2_raw, nc.scalar.copy)
+        w2_bf = round_weight("w2", [w2_raw], nc.scalar.copy)
 
         w3_mx = mx_tiles("w3")
         quantize(w3_mx, w3_bf)
-        z2_mx = scale_round_quantize("z2", rest, neg_gm)
+        z2_mx = scale_round_quantize("z2", rest, gm_sb)
         b_ps = product("b_ps", "hi", w3_mx, z2_mx)
         z_mx = scale_round_quantize("z", size, gn_sb)
         w2_mx = mx_tiles("w2")
@@ -171,13 +176,28 @@ def tile_picked_forkpullbkinddlse_none_p_kernel(
             nc.scalar.copy(a_win[t][:, S:], b_ps[t][:])
             nc.vector.tensor_tensor(gap[t][:], b_win[t][:].indirect(n6_sb[:]), a_win[t][:, S:], ALU.subtract)
         for t in range(PACK):
-            nc.scalar.activation(gate[t][:], gap[t][:], ACT.Sigmoid)
+            nc.scalar.activation(gate[t][:], gap[t][:], ACT.Sigmoid, scale=-1.0)
             nc.scalar.copy(a_win[t][:, :S], a_ps[t][:])
-        for t in range(PACK):
-            nc.vector.tensor_tensor(far[t][:], a_win[t][:].indirect(n5_sb[:]), gate[t][:], ALU.mult)
+        def finish(t, lo, hi, queue):
+            nc.vector.tensor_tensor(res[t][:, lo:hi], far[t][:, lo:hi], near[t][:, lo:hi], ALU.subtract)
+            queue.dma_start(out_rows[:, t, lo:hi], res[t][:, lo:hi])
+
+        def look_far(t, lo, hi):
+            nc.vector.tensor_tensor(
+                far[t][:, lo:hi], a_win[t][:].indirect(n5_sb[:, lo // 16 : hi // 16]), gate[t][:, lo:hi], ALU.mult
+            )
+
+        def look_near(t):
             nc.vector.scalar_tensor_tensor(near[t][:], gate[t][:], 1.0, a_win[t][:, :S], ALU.subtract, ALU.mult)
+
+        for t in range(3):
+            look_far(t, 0, S)
+            look_near(t)
             if t > 0:
-                nc.vector.tensor_tensor(res[t - 1][:], far[t - 1][:], near[t - 1][:], ALU.subtract)
-                nc.sync.dma_start(out_rows[:, t - 1, :], res[t - 1][:])
-        nc.vector.tensor_tensor(res[3][:], far[3][:], near[3][:], ALU.subtract)
-        nc.sync.dma_start(out_rows[:, 3, :], res[3][:])
+                finish(t - 1, 0, S, nc.sync)
+        look_near(3)
+        finish(2, 0, S, nc.sync)
+        look_far(3, 0, 256)
+        look_far(3, 256, S)
+        finish(3, 0, 256, nc.sync)
+        finish(3, 256, S, nc.scalar)

@@ -1,6 +1,7 @@
 from contextlib import ExitStack
 
 import concourse.mybir as mybir
+from concourse.masks import make_identity
 
 F32 = mybir.dt.float32
 BF16 = mybir.dt.bfloat16
@@ -88,6 +89,8 @@ def tile_picked_forkpullbkinddlse_none_p_kernel(
         tab_win = planes("tab_win", 2 * S)
         for t in range(PACK):
             nc.gpsimd.memset(tab_win[t][:, S:], 0.0)
+        ident = keep.tile([P, P], F32, name="ident")
+        make_identity(nc, ident[:])
         gn_sb = keep.tile([P, PACK], F32, name="gn_sb")
         gm_sb = keep.tile([P, PACK], F32, name="gm_sb")
         nc.gpsimd.dma_start(gn_sb[:], gn.rearrange("(p t) o -> p (t o)", t=PACK))
@@ -133,16 +136,17 @@ def tile_picked_forkpullbkinddlse_none_p_kernel(
         nc.vector.tensor_copy(b_win[1][:, S:], tab_win[1][:].indirect(n1_sb[:]))
         both = keep.tile([P, S], F32, name="both")
         for pair in ((0, 1), (2, 3)):
+            later = pair[::-1] if pair[0] == 0 else pair
             for t in pair:
                 nc.scalar.copy(y_win[t][:, :S], y_ps[t][:])
-            for t in pair:
+            for t in later:
                 nc.scalar.activation(y_win[t][:, S:], y_ps[t][:], ACT.Exp)
             for t in pair:
                 nc.scalar.activation(ex3[t][:], y_win[t][:].indirect(n3_sb[:]), ACT.Exp)
             for t in pair:
                 if t != 1:
                     nc.vector.tensor_tensor(b_win[t][:, S:], tab_win[t][:].indirect(n1_sb[:]), y_win[t][:, :S], ALU.subtract)
-            for t in pair:
+            for t in later:
                 dst = both[:] if t == 1 else diff[:, t, :]
                 nc.vector.tensor_tensor(dst, y_win[t][:].indirect(n2_sb[:]), b_win[t][:, S:], ALU.add)
             if pair[0] == 0:
@@ -177,7 +181,7 @@ def tile_picked_forkpullbkinddlse_none_p_kernel(
             nc.vector.tensor_tensor(gap[t][:], b_win[t][:].indirect(n6_sb[:]), a_win[t][:, S:], ALU.subtract)
         for t in range(PACK):
             nc.scalar.activation(gate[t][:], gap[t][:], ACT.Sigmoid, scale=-1.0)
-            nc.scalar.copy(a_win[t][:, :S], a_ps[t][:])
+            nc.scalar.activation(a_win[t][:, :S], a_ps[t][:], ACT.Copy, scale=-1.0 if t < 2 else 1.0)
         def finish(t, lo, hi, queue):
             nc.vector.tensor_tensor(res[t][:, lo:hi], far[t][:, lo:hi], near[t][:, lo:hi], ALU.subtract)
             queue.dma_start(out_rows[:, t, lo:hi], res[t][:, lo:hi])
@@ -188,13 +192,27 @@ def tile_picked_forkpullbkinddlse_none_p_kernel(
             )
 
         def look_near(t):
-            nc.vector.scalar_tensor_tensor(near[t][:], gate[t][:], 1.0, a_win[t][:, :S], ALU.subtract, ALU.mult)
+            nc.vector.scalar_tensor_tensor(near[t][:], gate[t][:], 1.0, a_ps[t][:], ALU.subtract, ALU.mult)
+
+        def finish_on_tensor(t):
+            turned = psum.tile([P, S], F32, name=f"turned{t}", tag=f"hi{2 * t}")
+            for c in range(S // P):
+                cols = slice(c * P, (c + 1) * P)
+                nc.tensor.matmul(turned[:, cols], far[t][:, cols], ident[:], is_transpose=True, start=True, stop=False)
+                nc.tensor.matmul(turned[:, cols], near[t][:, cols], ident[:], is_transpose=True, start=False, stop=True)
+            nc.scalar.copy(gap[t][:], turned[:])
+            back = psum.tile([P, S], F32, name=f"back{t}", tag=f"hi{2 * t + 1}")
+            for c in range(S // P):
+                cols = slice(c * P, (c + 1) * P)
+                nc.tensor.transpose(back[:, cols], gap[t][:, cols], ident[:])
+            nc.scalar.activation(res[t][:], back[:], ACT.Copy, scale=-1.0)
+            nc.sync.dma_start(out_rows[:, t, :], res[t][:])
 
         for t in range(3):
             look_far(t, 0, S)
             look_near(t)
-            if t > 0:
-                finish(t - 1, 0, S, nc.sync)
+            if t < 2:
+                finish_on_tensor(t)
         look_near(3)
         finish(2, 0, S, nc.sync)
         look_far(3, 0, 256)

@@ -160,6 +160,9 @@ def tile_picked_forkpullbkinddlse_none_p_kernel(
         nc.scalar.activation(size[:], diff[:], ACT.Abs)
         w2_bf = round_weight("w2", [w2_raw], nc.scalar.copy)
 
+        warm = keep.tile([P, 1], F32, name="warm")
+        nc.scalar.activation(warm[:], size[:, 0, 0:1], ACT.Sigmoid)
+
         w3_mx = mx_tiles("w3")
         quantize(w3_mx, w3_bf)
         z2_mx = scale_round_quantize("z2", rest, gm_sb)
@@ -195,17 +198,18 @@ def tile_picked_forkpullbkinddlse_none_p_kernel(
             nc.vector.scalar_tensor_tensor(near[t][:], gate[t][:], 1.0, a_ps[t][:], ALU.subtract, ALU.mult)
 
         def finish_on_tensor(t):
-            turned = psum.tile([P, S], F32, name=f"turned{t}", tag=f"hi{2 * t}")
-            for c in range(S // P):
-                cols = slice(c * P, (c + 1) * P)
-                nc.tensor.matmul(turned[:, cols], far[t][:, cols], ident[:], is_transpose=True, start=True, stop=False)
-                nc.tensor.matmul(turned[:, cols], near[t][:, cols], ident[:], is_transpose=True, start=False, stop=True)
-            nc.scalar.copy(gap[t][:], turned[:])
-            back = psum.tile([P, S], F32, name=f"back{t}", tag=f"hi{2 * t + 1}")
-            for c in range(S // P):
-                cols = slice(c * P, (c + 1) * P)
-                nc.tensor.transpose(back[:, cols], gap[t][:, cols], ident[:])
-            nc.scalar.activation(res[t][:], back[:], ACT.Copy, scale=-1.0)
+            for h in range(2):
+                lo = h * S // 2
+                blocks = [(slice(c * P, (c + 1) * P), slice(lo + c * P, lo + (c + 1) * P)) for c in range(2)]
+                turned = psum.tile([P, S // 2], F32, name=f"turned{t}{h}", tag=f"hi{2 * h}")
+                for here, cols in blocks:
+                    nc.tensor.matmul(turned[:, here], far[t][:, cols], ident[:], is_transpose=True, start=True, stop=False)
+                    nc.tensor.matmul(turned[:, here], near[t][:, cols], ident[:], is_transpose=True, start=False, stop=True)
+                nc.scalar.copy(gap[t][:, lo : lo + S // 2], turned[:])
+                back = psum.tile([P, S // 2], F32, name=f"back{t}{h}", tag=f"hi{2 * h + 1}")
+                for here, cols in blocks:
+                    nc.tensor.transpose(back[:, here], gap[t][:, cols], ident[:])
+                nc.scalar.activation(res[t][:, lo : lo + S // 2], back[:], ACT.Copy, scale=-1.0)
             nc.sync.dma_start(out_rows[:, t, :], res[t][:])
 
         for t in range(3):
@@ -218,4 +222,4 @@ def tile_picked_forkpullbkinddlse_none_p_kernel(
         look_far(3, 0, 256)
         look_far(3, 256, S)
         finish(3, 0, 256, nc.sync)
-        finish(3, 256, S, nc.scalar)
+        finish(3, 256, S, nc.sync)

@@ -88,7 +88,7 @@ def tile_picked_forkpullbkinddlse_none_p_kernel(
         nc.gpsimd.memset(xs_win[:].bitcast(I32), 0)
         tab_win = planes("tab_win", 2 * S)
         for t in range(PACK):
-            nc.gpsimd.memset(tab_win[t][:, S:], 0.0)
+            nc.vector.memset(tab_win[t][:, S:], 0.0)
         ident = keep.tile([P, P], F32, name="ident")
         make_identity(nc, ident[:])
         gn_sb = keep.tile([P, PACK], F32, name="gn_sb")
@@ -120,8 +120,15 @@ def tile_picked_forkpullbkinddlse_none_p_kernel(
         quantize(w1_mx, round_weight("w1", w1_raw, nc.vector.tensor_copy))
         x_mx = mx_tiles("x")
         nc.vector.tensor_copy(x_mx[1][:], xs_win[:].indirect(offs_sb[:]))
-        nc.vector.tensor_copy(x_mx[0][:], xw_win[:].indirect(offs_sb[:]))
-        y_ps = product("y_ps", "lo", w1_mx, x_mx)
+        for h in range(2):
+            nc.vector.tensor_copy(x_mx[0][:, h * 256 : (h + 1) * 256], xw_win[:].indirect(offs_sb[:, h * 16 : (h + 1) * 16]))
+        y_ps = [psum.tile([P, S], F32, name=f"y_ps{t}", tag=f"lo{t}") for t in range(PACK)]
+        for t, lo, hi in ((0, 0, 256), (1, 0, 256), (0, 256, S), (1, 256, S), (2, 0, S), (3, 0, S)):
+            cols = slice(t * P, (t + 1) * P)
+            nc.tensor.matmul_mx(
+                y_ps[t][:, lo:hi], w1_mx[0][:, cols].bitcast(FP8X4), w1_mx[1][:, cols],
+                x_mx[0][:, lo:hi].bitcast(FP8X4), x_mx[1][:, lo:hi], start=True, stop=True,
+            )
 
         y_win = planes("y_win", 2 * S)
         a_win = planes("a_win", 2 * S)

from contextlib import ExitStack

import concourse.mybir as mybir
from concourse.masks import make_identity

F32 = mybir.dt.float32
BF16 = mybir.dt.bfloat16
I32 = mybir.dt.int32
U32 = mybir.dt.uint32
U16 = mybir.dt.uint16
U8 = mybir.dt.uint8
FP8X4 = mybir.dt.float8_e4m3fn_x4
ALU = mybir.AluOpType
ACT = mybir.ActivationFunctionType

P = 128
PACK = 4
T = 2048
S = 512
W = 512
FLOPS = 3 * 2 * 512 * 512 * 512


def tile_picked_forkpullbkinddlse_none_p_kernel(
    tc, x_words, x_scales, w1, tab, gn, w2, gm, w3, offs, n1, n2, n3, n4, n5, n6, out
):
    nc = tc.nc
    with ExitStack() as ctx:
        keep = ctx.enter_context(tc.tile_pool(name="keep", bufs=1))
        psum = ctx.enter_context(tc.psum_pool(name="psum", bufs=1))

        def load_list(name, src):
            tile = keep.tile([P, S // 16], U16, name=name)
            nc.sync.dma_start(tile[:], src)
            return tile

        def planes(name, width):
            return [keep.tile([P, width], F32, name=f"{name}{t}") for t in range(PACK)]

        def load_weight(name, w):
            tile = keep.tile([P, PACK, w.shape[1]], F32, name=f"{name}_raw")
            nc.sync.dma_start(tile[:], w.rearrange("(p j) n -> p j n", j=PACK))
            return tile

        def round_weight(name, raw, copy):
            dealt = keep.tile([P, PACK * W], BF16, name=f"{name}_bf", align_bytes=64)
            view = dealt[:].rearrange("p (t m j) -> p m j t", t=PACK, j=PACK)
            span = P // len(raw)
            for h, tile in enumerate(raw):
                copy(view[:, h * span : (h + 1) * span], tile[:].rearrange("p j (m t) -> p m j t", t=PACK))
            return dealt

        def mx_tiles(name):
            codes = keep.tile([P, W], U32, name=f"{name}_codes", align_bytes=64)
            scales = keep.tile([P, W], U8, name=f"{name}_scales", align_bytes=64)
            return codes, scales

        def quantize(mx, values, lo=0, hi=W):
            nc.vector.quantize_mx(mx[0][:, lo:hi].bitcast(FP8X4), mx[1][:, lo:hi], values[:, PACK * lo : PACK * hi])

        def product(name, tag, weight, moving):
            banks = []
            for t in range(PACK):
                bank = psum.tile([P, S], F32, name=f"{name}{t}", tag=f"{tag}{t}")
                cols = slice(t * P, (t + 1) * P)
                nc.tensor.matmul_mx(
                    bank[:], weight[0][:, cols].bitcast(FP8X4), weight[1][:, cols],
                    moving[0][:].bitcast(FP8X4), moving[1][:], start=True, stop=True,
                )
                banks.append(bank)
            return banks

        def scale_round_quantize(name, values, gain):
            rounded = keep.tile([P, PACK * S], BF16, name=f"{name}_bf", align_bytes=64)
            mx = mx_tiles(name)
            src = values[:].rearrange("p t (c i) -> p c t i", i=4)
            dst = rounded[:].rearrange("p (c i t) -> p c t i", i=4, t=PACK)
            half = S // 8
            spread = gain[:].unsqueeze(1).unsqueeze(3).broadcast_to([P, half, PACK, 4])
            for h in range(2):
                c = slice(h * half, (h + 1) * half)
                nc.vector.tensor_tensor(dst[:, c], src[:, c], spread, ALU.mult)
            for h in range(2):
                quantize(mx, rounded, h * S // 2, (h + 1) * S // 2)
            return mx

        xs_win = keep.tile([P, T], U8, name="xs_win")
        nc.gpsimd.memset(xs_win[:].bitcast(I32), 0)
        tab_win = planes("tab_win", 2 * S)
        for t in range(PACK):
            nc.vector.memset(tab_win[t][:, S:], 0.0)
        ident = keep.tile([P, P], F32, name="ident")
        make_identity(nc, ident[:])
        gn_sb = keep.tile([P, PACK], F32, name="gn_sb")
        gm_sb = keep.tile([P, PACK], F32, name="gm_sb")
        nc.gpsimd.dma_start(gn_sb[:], gn.rearrange("(p t) o -> p (t o)", t=PACK))
        nc.gpsimd.dma_start(gm_sb[:], gm.rearrange("(p t) o -> p (t o)", t=PACK))

        w1_raw = [load_weight("w1a", w1[:, : W // 2])]
        for q in range(4):
            nc.sync.dma_start(xs_win[32 * q : 32 * q + 4, :].bitcast(I32), x_scales[0, 4 * q : 4 * q + 4, :].bitcast(I32))
        offs_sb = load_list("offs_sb", offs)
        w1_raw.append(load_weight("w1b", w1[:, W // 2 :]))
        xw_win = keep.tile([P, T], U32, name="xw_win")
        nc.sync.dma_start(xw_win[:].bitcast(I32), x_words[0].rearrange("p n t -> p (n t)").bitcast(I32))
        n1_sb = load_list("n1_sb", n1)
        n2_sb = load_list("n2_sb", n2)
        n3_sb = load_list("n3_sb", n3)
        tab_rows = tab.rearrange("(p t) n -> p t n", t=PACK)
        for t in (1, 0, 2, 3):
            nc.sync.dma_start(tab_win[t][:, :S], tab_rows[:, t, :])
        n4_sb = load_list("n4_sb", n4)
        w3_raw = load_weight("w3", w3)
        w2_raw = load_weight("w2", w2)
        n6_sb = load_list("n6_sb", n6)
        n5_sb = load_list("n5_sb", n5)


        w1_mx = mx_tiles("w1")
        quantize(w1_mx, round_weight("w1", w1_raw, nc.vector.tensor_copy))
        x_mx = mx_tiles("x")
        nc.vector.tensor_copy(x_mx[1][:], xs_win[:].indirect(offs_sb[:]))
        for h in range(2):
            nc.vector.tensor_copy(x_mx[0][:, h * 256 : (h + 1) * 256], xw_win[:].indirect(offs_sb[:, h * 16 : (h + 1) * 16]))
        y_ps = [psum.tile([P, S], F32, name=f"y_ps{t}", tag=f"lo{t}") for t in range(PACK)]
        for t, lo, hi in ((0, 0, 256), (1, 0, 256), (0, 256, S), (1, 256, S), (2, 0, S), (3, 0, S)):
            cols = slice(t * P, (t + 1) * P)
            nc.tensor.matmul_mx(
                y_ps[t][:, lo:hi], w1_mx[0][:, cols].bitcast(FP8X4), w1_mx[1][:, cols],
                x_mx[0][:, lo:hi].bitcast(FP8X4), x_mx[1][:, lo:hi], start=True, stop=True,
            )

        y_win = planes("y_win", 2 * S)
        a_win = planes("a_win", 2 * S)
        b_win = planes("b_win", 2 * S)
        lse = planes("lse", S)
        ex3 = planes("ex3", S)
        exsum = planes("exsum", S)
        diff = keep.tile([P, PACK, S], F32, name="diff")
        size = keep.tile([P, PACK, S], F32, name="size")
        rest = keep.tile([P, PACK, S], F32, name="rest")

        nc.vector.tensor_copy(b_win[1][:, S:], tab_win[1][:].indirect(n1_sb[:]))
        both = keep.tile([P, S], F32, name="both")
        for pair in ((0, 1), (2, 3)):
            later = pair[::-1] if pair[0] == 0 else pair
            for t in pair:
                nc.scalar.copy(y_win[t][:, :S], y_ps[t][:])
            for t in later:
                nc.scalar.activation(y_win[t][:, S:], y_ps[t][:], ACT.Exp)
            for t in pair:
                nc.scalar.activation(ex3[t][:], y_win[t][:].indirect(n3_sb[:]), ACT.Exp)
            for t in pair:
                if t != 1:
                    nc.vector.tensor_tensor(b_win[t][:, S:], tab_win[t][:].indirect(n1_sb[:]), y_win[t][:, :S], ALU.subtract)
            for t in later:
                dst = both[:] if t == 1 else diff[:, t, :]
                nc.vector.tensor_tensor(dst, y_win[t][:].indirect(n2_sb[:]), b_win[t][:, S:], ALU.add)
            if pair[0] == 0:
                nc.vector.tensor_tensor(diff[:, 1, :], both[:], y_win[1][:, :S], ALU.subtract)
            for t in pair:
                nc.vector.tensor_tensor(exsum[t][:], ex3[t][:], y_win[t][:, S:], ALU.add)
        for t in range(PACK):
            nc.scalar.activation(lse[t][:], exsum[t][:], ACT.Ln)
            nc.vector.tensor_tensor(rest[:, t, :], y_win[t][:].indirect(n4_sb[:]), lse[t][:], ALU.subtract)
        w3_bf = round_weight("w3", [w3_raw], nc.scalar.copy)
        nc.scalar.activation(size[:], diff[:], ACT.Abs)
        w2_bf = round_weight("w2", [w2_raw], nc.scalar.copy)

        warm = keep.tile([P, 1], F32, name="warm")
        nc.scalar.activation(warm[:], size[:, 0, 0:1], ACT.Sigmoid)

        w3_mx = mx_tiles("w3")
        quantize(w3_mx, w3_bf)
        z2_mx = scale_round_quantize("z2", rest, gm_sb)
        b_ps = product("b_ps", "hi", w3_mx, z2_mx)
        z_mx = scale_round_quantize("z", size, gn_sb)
        w2_mx = mx_tiles("w2")
        quantize(w2_mx, w2_bf)
        a_ps = product("a_ps", "lo", w2_mx, z_mx)

        gap = planes("gap", S)
        gate = planes("gate", S)
        far = planes("far", S)
        near = planes("near", S)
        res = planes("res", S)
        out_rows = out.rearrange("(p t) n -> p t n", t=PACK)
        for t in range(PACK):
            nc.scalar.copy(b_win[t][:, :S], b_ps[t][:])
            nc.scalar.copy(a_win[t][:, S:], b_ps[t][:])
            nc.vector.tensor_tensor(gap[t][:], b_win[t][:].indirect(n6_sb[:]), a_win[t][:, S:], ALU.subtract)
        for t in range(PACK):
            nc.scalar.activation(gate[t][:], gap[t][:], ACT.Sigmoid, scale=-1.0)
            nc.scalar.activation(a_win[t][:, :S], a_ps[t][:], ACT.Copy, scale=-1.0 if t < 2 else 1.0)
        def finish(t, lo, hi, queue):
            nc.vector.tensor_tensor(res[t][:, lo:hi], far[t][:, lo:hi], near[t][:, lo:hi], ALU.subtract)
            queue.dma_start(out_rows[:, t, lo:hi], res[t][:, lo:hi])

        def look_far(t, lo, hi):
            nc.vector.tensor_tensor(
                far[t][:, lo:hi], a_win[t][:].indirect(n5_sb[:, lo // 16 : hi // 16]), gate[t][:, lo:hi], ALU.mult
            )

        def look_near(t):
            nc.vector.scalar_tensor_tensor(near[t][:], gate[t][:], 1.0, a_ps[t][:], ALU.subtract, ALU.mult)

        def finish_on_tensor(t):
            for h in range(2):
                lo = h * S // 2
                blocks = [(slice(c * P, (c + 1) * P), slice(lo + c * P, lo + (c + 1) * P)) for c in range(2)]
                turned = psum.tile([P, S // 2], F32, name=f"turned{t}{h}", tag=f"hi{2 * h}")
                for here, cols in blocks:
                    nc.tensor.matmul(turned[:, here], far[t][:, cols], ident[:], is_transpose=True, start=True, stop=False)
                    nc.tensor.matmul(turned[:, here], near[t][:, cols], ident[:], is_transpose=True, start=False, stop=True)
                nc.scalar.copy(gap[t][:, lo : lo + S // 2], turned[:])
                back = psum.tile([P, S // 2], F32, name=f"back{t}{h}", tag=f"hi{2 * h + 1}")
                for here, cols in blocks:
                    nc.tensor.transpose(back[:, here], gap[t][:, cols], ident[:])
                nc.scalar.activation(res[t][:, lo : lo + S // 2], back[:], ACT.Copy, scale=-1.0)
            nc.sync.dma_start(out_rows[:, t, :], res[t][:])

        for t in range(3):
            look_far(t, 0, S)
            look_near(t)
            if t < 2:
                finish_on_tensor(t)
        look_near(3)
        finish(2, 0, S, nc.sync)
        look_far(3, 0, 256)
        look_far(3, 256, S)
        finish(3, 0, 256, nc.sync)
        finish(3, 256, S, nc.sync)
